import numpy as np
import ml_dtypes


def mxq(x, axis, fmt="e4m3"):
    dtype, down = {"e4m3": (ml_dtypes.float8_e4m3fn, 7), "e5m2": (ml_dtypes.float8_e5m2, 14)}[fmt]
    v = np.moveaxis(np.asarray(x, np.float32).astype(ml_dtypes.bfloat16).astype(np.float64), axis, -1)
    blocks = v.reshape(v.shape[:-1] + (-1, 32))
    amax = np.abs(blocks).max(-1, keepdims=True)
    byte = np.maximum(np.where(amax > 0, np.frexp(amax)[1] - 1 + 127, 0) - down, 1)
    scale = np.exp2(byte - 127.0)
    codes = (blocks / scale).astype(np.float32).astype(dtype).astype(np.float64)
    return np.moveaxis((codes * scale).reshape(v.shape), -1, axis)


WIDE = False


def mx_kscale(k):
    if not WIDE:
        return np.ones(k)
    levels = np.array([30, -30])
    if k % 512:
        return np.exp2(np.random.permutation(np.resize(levels, k // 32))).repeat(32)
    a = np.empty((k // 512, 16))
    for p in range(k // 512):
        a[p, :8] = np.random.permutation(np.resize(levels, 8))
        for g in range(8):
            far = levels[np.abs(levels - a[p, g]) >= 10]
            a[p, g + 8] = far[np.random.randint(len(far))]
    return np.exp2(a.ravel()).repeat(32)


def f64(x):
    return np.asarray(x).astype(np.float64)


def striped(idx):
    return np.tile(np.asarray(idx).reshape(-1, 16).T, (8, 1)).astype(np.uint16)


def unstriped(offs):
    return offs[:16].T.reshape(-1).astype(np.int64)


E2M1 = np.array([0.0, 0.5, 1.0, 1.5, 2.0, 3.0, 4.0, 6.0, -0.0, -0.5, -1.0, -1.5, -2.0, -3.0, -4.0, -6.0])


def pack_weight(w, fmt):
    k, n = w.shape
    w = f64(np.asarray(w, np.float32).astype(ml_dtypes.bfloat16)).reshape(k // 32, 32, n)
    amax = np.abs(w).max(1)
    if fmt == "e4m3":
        byte = np.frexp(amax)[1] - 1 + 127 - 7
    else:
        mant, ex = np.frexp(amax / 6.0)
        byte = np.where(mant > 0.5, ex, ex - 1) + 127
    byte = np.clip(np.where(amax > 0, byte, 1), 1, 254)
    scaled = (w * np.exp2(127.0 - byte)[:, None, :]).reshape(k, n).astype(np.float32)
    by_word = np.ascontiguousarray(scaled.reshape(k // 512, 128, 4, n).transpose(0, 1, 3, 2))
    if fmt == "e4m3":
        words = by_word.astype(ml_dtypes.float8_e4m3fn).view(np.uint8)
    else:
        c = by_word.astype(ml_dtypes.float4_e2m1fn).view(np.uint8) & 0xF
        words = (c[..., 0::2] | (c[..., 1::2] << 4)).reshape(k // 512, 128, 2 * n)
    return np.ascontiguousarray(words), np.ascontiguousarray(byte.astype(np.uint8).reshape(k // 512, 16, n))


def unpack_weight(words, scales, fmt):
    g, _, n = scales.shape
    words = np.ascontiguousarray(words).reshape(g, 128, n, -1)
    if fmt == "e4m3":
        vals = words.view(ml_dtypes.float8_e4m3fn).astype(np.float64)
    else:
        nib = np.empty((g, 128, n, 4), np.uint8)
        nib[..., 0::2] = words & 0xF
        nib[..., 1::2] = words >> 4
        vals = E2M1[nib]
    vals = vals * np.repeat(np.exp2(scales.astype(np.float64) - 127.0), 8, axis=1)[..., None]
    return vals.transpose(0, 1, 3, 2).reshape(g * 512, n)


K, T, J, R, N, Z = 1024, 1024, 256, 512, 256, 512


def setup_inputs():
    n = np.random.standard_normal
    idx = np.random.permutation(T)[:J]
    idx2 = np.random.permutation(T)[:J]
    idx3 = np.random.permutation(Z)[:J]
    fk = mx_kscale(K)
    fr = mx_kscale(R)
    wp = pack_weight(n((K, R)) * 1 / np.sqrt(K) * fk[:, None] * fr, "e2m1")
    wbp = pack_weight(n((R, N)) * 1 / np.sqrt(R) / fr[:, None], "e4m3")
    return {
        "xf": (n((K, T))).astype(np.float32),
        "fk": (np.random.uniform(0.5, 2.0, (K, 1)) / fk[:, None]).astype(np.float32),
        "w_words": wp[0],
        "w_scales": wp[1],
        "wb_words": wbp[0],
        "wb_scales": wbp[1],
        "tz": (n((N, Z)) * 0.6).astype(np.float32),
        "rw": (np.random.uniform(0.5, 2.0, (1, J))).astype(np.float32),
        "offs": striped(idx),
        "offs2": striped(idx2),
        "offs3": striped(idx3),
    }


def reference(xf, fk, w_words, w_scales, wb_words, wb_scales, tz, rw, offs, offs2, offs3):
    idx = unstriped(offs)
    idx2 = unstriped(offs2)
    idx3 = unstriped(offs3)
    wu = unpack_weight(w_words, w_scales, "e2m1")
    wbu = unpack_weight(wb_words, wb_scales, "e4m3")
    u = np.maximum(f64(xf)[:, idx], f64(xf)[:, idx2]) * f64(fk)
    uq = mxq(u, 0, "e4m3")
    a = wu.T @ uq
    hid = np.maximum(a, 0.0)
    hidq = mxq(hid, 0, "e5m2")
    p = wbu.T @ hidq
    y = np.maximum(p, f64(tz)[:, idx3]) * f64(rw)
    return y

@@ -1,0 +1,220 @@
+from contextlib import ExitStack
+
+import concourse.mybir as mybir
+from concourse.masks import make_identity
+
+K, T, J, R, N, Z = 1024, 1024, 256, 512, 256, 512
+FLOPS = 2 * K * R * J + 2 * R * N * J
+
+F32 = mybir.dt.float32
+BF16 = mybir.dt.bfloat16
+I32 = mybir.dt.int32
+U32 = mybir.dt.uint32
+U16 = mybir.dt.uint16
+U8 = mybir.dt.uint8
+E4M3 = mybir.dt.float8_e4m3fn_x4
+E5M2 = mybir.dt.float8_e5m2_x4
+E2M1 = mybir.dt.float4_e2m1fn_x4
+MAX = mybir.AluOpType.max
+MULT = mybir.AluOpType.mult
+COPY = mybir.ActivationFunctionType.Copy
+RELU = mybir.ActivationFunctionType.Relu
+
+P = 128
+PACK = 4
+PASSES = K // (P * PACK)
+HALVES = 2
+JH = J // HALVES
+LIST_COLS = J // 16
+HALF_COLS = JH // 16
+N_TILES = N // P
+VECTOR_PLANES = (0, 4)
+
+
+def tile_list_largerpicks_plain_floored_kernel(
+    tc, xf, fk, w_words, w_scales, wb_words, wb_scales, tz, rw, offs, offs2, offs3, out
+):
+    nc = tc.nc
+    with ExitStack() as ctx:
+        keep = ctx.enter_context(tc.tile_pool(name="keep", bufs=1))
+        psum = ctx.enter_context(tc.psum_pool(name="psum", bufs=1))
+
+        def sbuf(shape, dtype, name, tag=None):
+            return keep.tile(shape, dtype, name=name, tag=tag or name, align_bytes=64)
+
+        list1 = sbuf([P, LIST_COLS], U16, "list1")
+        list2 = sbuf([P, LIST_COLS], U16, "list2")
+        list3 = sbuf([P, LIST_COLS], U16, "list3")
+        w_raw = sbuf([P, PASSES, 2 * R], U8, "w_raw")
+        ws_raw = sbuf([P, PASSES, R], U8, "ws_raw")
+        w_dealt = sbuf([P, PASSES, 2 * R], U8, "w_dealt")
+        wb_codes = sbuf([P, N], U32, "wb_codes")
+        wb_sc = sbuf([P, N], U8, "wb_sc")
+        fk_sb = sbuf([P, PASSES, PACK], F32, "fk_sb")
+        rw_col = sbuf([P, 2], F32, "rw_col")
+        ident = sbuf([P, P], F32, "ident")
+        planes = [sbuf([P, T], F32, f"plane{q}") for q in range(PASSES * PACK)]
+        tz_sb = [sbuf([P, Z], F32, f"tz{n}") for n in range(N_TILES)]
+
+        nc.gpsimd.memset(ws_raw[:].rearrange("p a r -> p (a r)").bitcast(I32), 0)
+        nc.vector.memset(wb_sc[:].bitcast(I32), 0)
+        make_identity(nc, ident[:])
+
+        x_rows = xf.rearrange("(a p i) t -> a i p t", p=P, i=PACK)
+
+        def load_plane(q):
+            nc.sync.dma_start(out=planes[q][:], in_=x_rows[q // PACK, q % PACK])
+
+        def load_w_scales(quad):
+            nc.sync.dma_start(
+                out=ws_raw[32 * quad : 32 * quad + 4].bitcast(I32),
+                in_=w_scales[:, 4 * quad : 4 * quad + 4, :].rearrange("a r c -> r a c").bitcast(I32),
+            )
+
+        def load_tz(n):
+            nc.sync.dma_start(out=tz_sb[n][:], in_=tz[n * P : (n + 1) * P, :])
+
+        nc.sync.dma_start(list1[:], offs)
+        nc.sync.dma_start(list2[:], offs2)
+        load_plane(0)
+        nc.sync.dma_start(out=w_raw[:].bitcast(I32), in_=w_words.rearrange("a p c -> p a c").bitcast(I32))
+        nc.sync.dma_start(out=fk_sb[:], in_=fk.rearrange("(a p i) o -> p a (i o)", p=P, i=PACK))
+        for q in range(1, PACK):
+            load_plane(q)
+        load_w_scales(0)
+        load_w_scales(1)
+        load_plane(PACK)
+        load_w_scales(2)
+        load_w_scales(3)
+        for q in range(PACK + 1, PASSES * PACK):
+            load_plane(q)
+        nc.sync.dma_start(list3[:], offs3)
+        load_tz(0)
+        nc.sync.dma_start(
+            out=wb_codes[:].bitcast(I32), in_=wb_words[0].rearrange("p n t -> p (n t)").bitcast(I32)
+        )
+        load_tz(1)
+        with nc.allow_non_contiguous_dma(reason="one weight to a partition"):
+            nc.sync.dma_start(out=rw_col[:], in_=rw.rearrange("o (h p) -> p (o h)", p=P))
+        for quad in range(4):
+            nc.sync.dma_start(
+                out=wb_sc[32 * quad : 32 * quad + 4, :].bitcast(I32),
+                in_=wb_scales[0, 4 * quad : 4 * quad + 4, :].bitcast(I32),
+            )
+
+        nc.vector.tensor_copy(
+            out=w_dealt[:].bitcast(U16).rearrange("p a (t m) -> p a t m", t=PACK),
+            in_=w_raw[:].bitcast(U16).rearrange("p a (m t) -> p a t m", t=PACK),
+        )
+
+        acc = [psum.tile([P, PACK, JH], F32, name=f"acc{h}") for h in range(HALVES)]
+        prod = [psum.tile([P, N_TILES, JH], F32, name=f"prod{h}") for h in range(HALVES)]
+
+        u_il = [sbuf([P, J * PACK], BF16, f"u_il{a}") for a in range(PASSES)]
+        u_codes = [sbuf([P, J], U32, f"u_codes{a}") for a in range(PASSES)]
+        u_sc = [sbuf([P, J], U8, f"u_sc{a}") for a in range(PASSES)]
+
+        def gather(on_vector, dst, window, offsets):
+            if on_vector:
+                nc.vector.tensor_copy(dst, window[:].indirect(offsets))
+            else:
+                nc.scalar.activation(dst, window[:].indirect(offsets), COPY)
+
+        def scale_into(q, cols, larger):
+            a, i = divmod(q, PACK)
+            dst = u_il[a][:].rearrange("p (j i) -> p j i", i=PACK)[:, cols, i]
+            nc.vector.tensor_scalar_mul(dst, larger, fk_sb[:, a, i : i + 1])
+
+        def quantise_u(a, cols):
+            nc.vector.quantize_mx(
+                out=u_codes[a][:, cols].bitcast(E4M3),
+                scales=u_sc[a][:, cols],
+                in_=u_il[a][:, cols.start * PACK : cols.stop * PACK],
+            )
+
+        def first_product(a, h, ws_dealt):
+            for t in range(PACK):
+                nc.tensor.matmul_mx(
+                    out=acc[h][:, t, :],
+                    lhsT=w_dealt[:, a, 2 * P * t : 2 * P * (t + 1)].bitcast(E2M1),
+                    lhsT_scale=ws_dealt[:, a, P * t : P * (t + 1)],
+                    rhs=u_codes[a][:, half[h]].bitcast(E4M3),
+                    rhs_scale=u_sc[a][:, half[h]],
+                    start=(a == 0 and t == 0),
+                    stop=(a == PASSES - 1 and t == PACK - 1),
+                )
+
+        half = [slice(h * JH, (h + 1) * JH) for h in range(HALVES)]
+        whole = slice(0, J)
+        last = PASSES * PACK - 1
+        for q in range(last):
+            g1 = sbuf([P, J], F32, f"g1_{q}")
+            g2 = sbuf([P, J], F32, f"g2_{q}")
+            larger = sbuf([P, J], F32, f"larger{q}")
+            gather(False, g2[:], planes[q], list2[:])
+            gather(q in VECTOR_PLANES, g1[:], planes[q], list1[:])
+            nc.vector.tensor_tensor(larger[:], g1[:], g2[:], MAX)
+            scale_into(q, whole, larger[:])
+            if q == PACK - 1:
+                quantise_u(0, whole)
+            if q == PACK:
+                ws_dealt = sbuf([P, PASSES, R], U8, "ws_dealt", tag=f"larger{q}")
+                nc.vector.tensor_copy(
+                    out=ws_dealt[:].rearrange("p a (t m) -> p a t m", t=PACK),
+                    in_=ws_raw[:].rearrange("p a (m t) -> p a t m", t=PACK),
+                )
+                for h in range(HALVES):
+                    first_product(0, h, ws_dealt)
+
+        def half_list(lst, h):
+            return lst[:, h * HALF_COLS : (h + 1) * HALF_COLS]
+
+        g1_last = sbuf([P, J], F32, "g1_last", tag=f"g1_{last - 1}")
+        g2_last = sbuf([P, J], F32, "g2_last")
+        larger = sbuf([P, J], F32, "larger_last")
+        for h in range(HALVES):
+            gather(False, g2_last[:, half[h]], planes[last], half_list(list2, h))
+            gather(True, g1_last[:, half[h]], planes[last], half_list(list1, h))
+        for h in range(HALVES):
+            nc.vector.tensor_tensor(larger[:, half[h]], g1_last[:, half[h]], g2_last[:, half[h]], MAX)
+        for h in range(HALVES):
+            scale_into(last, half[h], larger[:, half[h]])
+        for h in range(HALVES):
+            quantise_u(PASSES - 1, half[h])
+            first_product(PASSES - 1, h, ws_dealt)
+
+        floor = sbuf([P, N_TILES, J], F32, "floor", tag=f"g2_{last - 1}")
+        for n in range(N_TILES):
+            gather(False, floor[:, n, :], tz_sb[n], list3[:])
+
+        out_rows = out.rearrange("(n p) j -> p n j", p=P)
+        for h in range(HALVES):
+            hid_il = sbuf([P, JH, PACK], BF16, f"hid_il{h}")
+            hid_codes = sbuf([P, JH], U32, f"hid_codes{h}")
+            hid_sc = sbuf([P, JH], U8, f"hid_sc{h}")
+            top = sbuf([P, N_TILES, JH], F32, f"top{h}")
+            res = sbuf([P, N_TILES, JH], F32, f"res{h}")
+            nc.scalar.activation(hid_il[:], acc[h][:].rearrange("p t j -> p j t"), RELU)
+            if h == 0:
+                rw_ps = psum.tile([P, HALVES, JH], F32, name="rw_ps", tag="acc0")
+                for c in range(HALVES):
+                    nc.tensor.transpose(rw_ps[:, c, :], rw_col[:, c : c + 1].to_broadcast([P, P]), ident[:])
+            nc.vector.quantize_mx(
+                out=hid_codes[:].bitcast(E5M2),
+                scales=hid_sc[:],
+                in_=hid_il[:].rearrange("p j t -> p (j t)"),
+            )
+            for n in range(N_TILES):
+                nc.tensor.matmul_mx(
+                    out=prod[h][:, n, :],
+                    lhsT=wb_codes[:, n * P : (n + 1) * P].bitcast(E4M3),
+                    lhsT_scale=wb_sc[:, n * P : (n + 1) * P],
+                    rhs=hid_codes[:].bitcast(E5M2),
+                    rhs_scale=hid_sc[:],
+                    start=True,
+                    stop=True,
+                )
+            nc.vector.tensor_tensor(top[:], prod[h][:], floor[:, :, half[h]], MAX)
+            weight = rw_ps[:, h, :].unsqueeze(1).to_broadcast([P, N_TILES, JH])
+            nc.vector.tensor_tensor(res[:], top[:], weight, MULT)
+            nc.sync.dma_start(out=out_rows[:, :, h * JH : (h + 1) * JH], in_=res[:])

@@ -28,7 +28,7 @@ JH = J // HALVES
 LIST_COLS = J // 16
 HALF_COLS = JH // 16
 N_TILES = N // P
-VECTOR_PLANES = (0, 4)
+VECTOR_PLANES = (2,)
 
 
 def tile_list_largerpicks_plain_floored_kernel(
@@ -54,10 +54,13 @@ def tile_list_largerpicks_plain_floored_kernel(
         rw_col = sbuf([P, 2], F32, "rw_col")
         ident = sbuf([P, P], F32, "ident")
         planes = [sbuf([P, T], F32, f"plane{q}") for q in range(PASSES * PACK)]
-        tz_sb = [sbuf([P, Z], F32, f"tz{n}") for n in range(N_TILES)]
+        tz_sb = sbuf([P, N_TILES, Z], F32, "tz_sb")
 
         nc.gpsimd.memset(ws_raw[:].rearrange("p a r -> p (a r)").bitcast(I32), 0)
         nc.vector.memset(wb_sc[:].bitcast(I32), 0)
+        warm = sbuf([P, 8], F32, "warm")
+        nc.vector.memset(warm[:, 0:4], 0.0)
+        nc.scalar.activation(warm[:, 4:8], warm[:, 0:4], COPY)
         make_identity(nc, ident[:])
 
         x_rows = xf.rearrange("(a p i) t -> a i p t", p=P, i=PACK)
@@ -71,9 +74,6 @@ def tile_list_largerpicks_plain_floored_kernel(
                 in_=w_scales[:, 4 * quad : 4 * quad + 4, :].rearrange("a r c -> r a c").bitcast(I32),
             )
 
-        def load_tz(n):
-            nc.sync.dma_start(out=tz_sb[n][:], in_=tz[n * P : (n + 1) * P, :])
-
         nc.sync.dma_start(list1[:], offs)
         nc.sync.dma_start(list2[:], offs2)
         load_plane(0)
@@ -81,19 +81,15 @@ def tile_list_largerpicks_plain_floored_kernel(
         nc.sync.dma_start(out=fk_sb[:], in_=fk.rearrange("(a p i) o -> p a (i o)", p=P, i=PACK))
         for q in range(1, PACK):
             load_plane(q)
-        load_w_scales(0)
-        load_w_scales(1)
-        load_plane(PACK)
-        load_w_scales(2)
-        load_w_scales(3)
-        for q in range(PACK + 1, PASSES * PACK):
+        for quad in range(4):
+            load_w_scales(quad)
+        for q in range(PACK, PASSES * PACK):
             load_plane(q)
         nc.sync.dma_start(list3[:], offs3)
-        load_tz(0)
+        nc.sync.dma_start(out=tz_sb[:], in_=tz.rearrange("(n p) z -> p n z", p=P))
         nc.sync.dma_start(
             out=wb_codes[:].bitcast(I32), in_=wb_words[0].rearrange("p n t -> p (n t)").bitcast(I32)
         )
-        load_tz(1)
         with nc.allow_non_contiguous_dma(reason="one weight to a partition"):
             nc.sync.dma_start(out=rw_col[:], in_=rw.rearrange("o (h p) -> p (o h)", p=P))
         for quad in range(4):
@@ -108,7 +104,7 @@ def tile_list_largerpicks_plain_floored_kernel(
         )
 
         acc = [psum.tile([P, PACK, JH], F32, name=f"acc{h}") for h in range(HALVES)]
-        prod = [psum.tile([P, N_TILES, JH], F32, name=f"prod{h}") for h in range(HALVES)]
+        prod = [[psum.tile([P, JH], F32, name=f"prod{h}_{n}") for n in range(N_TILES)] for h in range(HALVES)]
 
         u_il = [sbuf([P, J * PACK], BF16, f"u_il{a}") for a in range(PASSES)]
         u_codes = [sbuf([P, J], U32, f"u_codes{a}") for a in range(PASSES)]
@@ -116,9 +112,9 @@ def tile_list_largerpicks_plain_floored_kernel(
 
         def gather(on_vector, dst, window, offsets):
             if on_vector:
-                nc.vector.tensor_copy(dst, window[:].indirect(offsets))
+                nc.vector.tensor_copy(dst, window.indirect(offsets))
             else:
-                nc.scalar.activation(dst, window[:].indirect(offsets), COPY)
+                nc.scalar.activation(dst, window.indirect(offsets), COPY)
 
         def scale_into(q, cols, larger):
             a, i = divmod(q, PACK)
@@ -147,53 +143,77 @@ def tile_list_largerpicks_plain_floored_kernel(
         half = [slice(h * JH, (h + 1) * JH) for h in range(HALVES)]
         whole = slice(0, J)
         last = PASSES * PACK - 1
-        for q in range(last):
-            g1 = sbuf([P, J], F32, f"g1_{q}")
-            g2 = sbuf([P, J], F32, f"g2_{q}")
-            larger = sbuf([P, J], F32, f"larger{q}")
-            gather(False, g2[:], planes[q], list2[:])
-            gather(q in VECTOR_PLANES, g1[:], planes[q], list1[:])
-            nc.vector.tensor_tensor(larger[:], g1[:], g2[:], MAX)
-            scale_into(q, whole, larger[:])
-            if q == PACK - 1:
-                quantise_u(0, whole)
-            if q == PACK:
-                ws_dealt = sbuf([P, PASSES, R], U8, "ws_dealt", tag=f"larger{q}")
-                nc.vector.tensor_copy(
-                    out=ws_dealt[:].rearrange("p a (t m) -> p a t m", t=PACK),
-                    in_=ws_raw[:].rearrange("p a (m t) -> p a t m", t=PACK),
-                )
-                for h in range(HALVES):
-                    first_product(0, h, ws_dealt)
-
         def half_list(lst, h):
             return lst[:, h * HALF_COLS : (h + 1) * HALF_COLS]
 
-        g1_last = sbuf([P, J], F32, "g1_last", tag=f"g1_{last - 1}")
-        g2_last = sbuf([P, J], F32, "g2_last")
-        larger = sbuf([P, J], F32, "larger_last")
+        g1, g2, larger = {}, {}, {}
+
+        def pick(q):
+            g2[q] = sbuf([P, J], F32, f"g2_{q}")
+            g1[q] = sbuf([P, J], F32, f"g1_{q}", tag=f"g2_{q - 2}" if q in VECTOR_PLANES or q == last else None)
+            if q == last:
+                for h in range(HALVES):
+                    gather(False, g2[q][:, half[h]], planes[q][:], half_list(list2, h))
+                    gather(h == 0, g1[q][:, half[h]], planes[q][:], half_list(list1, h))
+            else:
+                gather(False, g2[q][:], planes[q][:], list2[:])
+                gather(q in VECTOR_PLANES, g1[q][:], planes[q][:], list1[:])
+
+        def keep_larger(q, pieces):
+            if q not in larger:
+                larger[q] = sbuf([P, J], F32, f"larger{q}")
+            for cols in pieces:
+                nc.vector.tensor_tensor(larger[q][:, cols], g1[q][:, cols], g2[q][:, cols], MAX)
+
+        def scale(q, pieces):
+            for cols in pieces:
+                scale_into(q, cols, larger[q][:, cols])
+
+        pick(0)
+        keep_larger(0, [whole])
+        scale(0, [whole])
+        pick(1)
+        pick(2)
+        keep_larger(1, [whole])
+        keep_larger(2, [whole])
+        scale(1, [whole])
+        scale(2, [whole])
+        pick(3)
+        keep_larger(3, [whole])
+        ws_dealt = sbuf([P, PASSES, R], U8, "ws_dealt", tag="larger2")
+        nc.vector.tensor_copy(
+            out=ws_dealt[:].rearrange("p a (t m) -> p a t m", t=PACK),
+            in_=ws_raw[:].rearrange("p a (m t) -> p a t m", t=PACK),
+        )
+        scale(3, [whole])
+        quantise_u(0, whole)
         for h in range(HALVES):
-            gather(False, g2_last[:, half[h]], planes[last], half_list(list2, h))
-            gather(True, g1_last[:, half[h]], planes[last], half_list(list1, h))
-        for h in range(HALVES):
-            nc.vector.tensor_tensor(larger[:, half[h]], g1_last[:, half[h]], g2_last[:, half[h]], MAX)
-        for h in range(HALVES):
-            scale_into(last, half[h], larger[:, half[h]])
+            first_product(0, h, ws_dealt)
+        pick(4)
+        keep_larger(4, [whole])
+        scale(4, [whole])
+        pick(5)
+        keep_larger(5, [whole])
+        scale(5, [whole])
+        pick(6)
+        pick(last)
+        keep_larger(6, [whole])
+        keep_larger(last, half[:1])
+        scale(6, [whole])
+        keep_larger(last, half[1:])
+        scale(last, half)
         for h in range(HALVES):
             quantise_u(PASSES - 1, half[h])
             first_product(PASSES - 1, h, ws_dealt)
 
         floor = sbuf([P, N_TILES, J], F32, "floor", tag=f"g2_{last - 1}")
         for n in range(N_TILES):
-            gather(False, floor[:, n, :], tz_sb[n], list3[:])
+            gather(False, floor[:, n, :], tz_sb[:, n, :], list3[:])
 
-        out_rows = out.rearrange("(n p) j -> p n j", p=P)
         for h in range(HALVES):
             hid_il = sbuf([P, JH, PACK], BF16, f"hid_il{h}")
             hid_codes = sbuf([P, JH], U32, f"hid_codes{h}")
             hid_sc = sbuf([P, JH], U8, f"hid_sc{h}")
-            top = sbuf([P, N_TILES, JH], F32, f"top{h}")
-            res = sbuf([P, N_TILES, JH], F32, f"res{h}")
             nc.scalar.activation(hid_il[:], acc[h][:].rearrange("p t j -> p j t"), RELU)
             if h == 0:
                 rw_ps = psum.tile([P, HALVES, JH], F32, name="rw_ps", tag="acc0")
@@ -206,7 +226,7 @@ def tile_list_largerpicks_plain_floored_kernel(
             )
             for n in range(N_TILES):
                 nc.tensor.matmul_mx(
-                    out=prod[h][:, n, :],
+                    out=prod[h][n][:],
                     lhsT=wb_codes[:, n * P : (n + 1) * P].bitcast(E4M3),
                     lhsT_scale=wb_sc[:, n * P : (n + 1) * P],
                     rhs=hid_codes[:].bitcast(E5M2),
@@ -214,7 +234,13 @@ def tile_list_largerpicks_plain_floored_kernel(
                     start=True,
                     stop=True,
                 )
-            nc.vector.tensor_tensor(top[:], prod[h][:], floor[:, :, half[h]], MAX)
-            weight = rw_ps[:, h, :].unsqueeze(1).to_broadcast([P, N_TILES, JH])
-            nc.vector.tensor_tensor(res[:], top[:], weight, MULT)
-            nc.sync.dma_start(out=out_rows[:, :, h * JH : (h + 1) * JH], in_=res[:])
+
+        for h in range(HALVES):
+            top = sbuf([P, N_TILES, JH], F32, f"top{h}")
+            res = [sbuf([P, JH], F32, f"res{h}_{n}") for n in range(N_TILES)]
+            for n in range(N_TILES):
+                nc.vector.tensor_tensor(top[:, n, :], prod[h][n][:], floor[:, n, half[h]], MAX)
+            for n in range(N_TILES):
+                nc.vector.tensor_tensor(res[n][:], top[:, n, :], rw_ps[:, h, :], MULT)
+                queue = nc.sync if n == 0 else nc.scalar
+                queue.dma_start(out=out[n * P : (n + 1) * P, half[h]], in_=res[n][:])

@@ -28,7 +28,7 @@ JH = J // HALVES
 LIST_COLS = J // 16
 HALF_COLS = JH // 16
 N_TILES = N // P
-VECTOR_PLANES = (2,)
+VECTOR_PLANES = 2
 
 
 def tile_list_largerpicks_plain_floored_kernel(
@@ -74,24 +74,23 @@ def tile_list_largerpicks_plain_floored_kernel(
                 in_=w_scales[:, 4 * quad : 4 * quad + 4, :].rearrange("a r c -> r a c").bitcast(I32),
             )
 
+        nc.sync.dma_start(out=w_raw[:].bitcast(I32), in_=w_words.rearrange("a p c -> p a c").bitcast(I32))
         nc.sync.dma_start(list1[:], offs)
         nc.sync.dma_start(list2[:], offs2)
-        load_plane(0)
-        nc.sync.dma_start(out=w_raw[:].bitcast(I32), in_=w_words.rearrange("a p c -> p a c").bitcast(I32))
-        nc.sync.dma_start(out=fk_sb[:], in_=fk.rearrange("(a p i) o -> p a (i o)", p=P, i=PACK))
-        for q in range(1, PACK):
+        nc.scalar.dma_start(out=fk_sb[:], in_=fk.rearrange("(a p i) o -> p a (i o)", p=P, i=PACK))
+        with nc.allow_non_contiguous_dma(reason="one weight to a partition"):
+            nc.scalar.dma_start(out=rw_col[:], in_=rw.rearrange("o (h p) -> p (o h)", p=P))
+        for q in range(3):
             load_plane(q)
         for quad in range(4):
             load_w_scales(quad)
-        for q in range(PACK, PASSES * PACK):
+        for q in range(3, PASSES * PACK):
             load_plane(q)
         nc.sync.dma_start(list3[:], offs3)
         nc.sync.dma_start(out=tz_sb[:], in_=tz.rearrange("(n p) z -> p n z", p=P))
         nc.sync.dma_start(
             out=wb_codes[:].bitcast(I32), in_=wb_words[0].rearrange("p n t -> p (n t)").bitcast(I32)
         )
-        with nc.allow_non_contiguous_dma(reason="one weight to a partition"):
-            nc.sync.dma_start(out=rw_col[:], in_=rw.rearrange("o (h p) -> p (o h)", p=P))
         for quad in range(4):
             nc.sync.dma_start(
                 out=wb_sc[32 * quad : 32 * quad + 4, :].bitcast(I32),
@@ -106,8 +105,15 @@ def tile_list_largerpicks_plain_floored_kernel(
         acc = [psum.tile([P, PACK, JH], F32, name=f"acc{h}") for h in range(HALVES)]
         prod = [[psum.tile([P, JH], F32, name=f"prod{h}_{n}") for n in range(N_TILES)] for h in range(HALVES)]
 
+        rw_ps = psum.tile([P, HALVES, JH], F32, name="rw_ps")
+        for h in range(HALVES):
+            nc.tensor.transpose(rw_ps[:, h, :], rw_col[:, h : h + 1].to_broadcast([P, P]), ident[:])
+
+        rw_first = sbuf([P, JH], F32, "rw_first")
+        nc.scalar.copy(rw_first[:], rw_ps[:, 0, :])
+
         u_il = [sbuf([P, J * PACK], BF16, f"u_il{a}") for a in range(PASSES)]
-        u_codes = [sbuf([P, J], U32, f"u_codes{a}") for a in range(PASSES)]
+        u_codes = {}
         u_sc = [sbuf([P, J], U8, f"u_sc{a}") for a in range(PASSES)]
 
         def gather(on_vector, dst, window, offsets):
@@ -143,25 +149,25 @@ def tile_list_largerpicks_plain_floored_kernel(
         half = [slice(h * JH, (h + 1) * JH) for h in range(HALVES)]
         whole = slice(0, J)
         last = PASSES * PACK - 1
-        def half_list(lst, h):
-            return lst[:, h * HALF_COLS : (h + 1) * HALF_COLS]
+        def halves_of(lst):
+            return [lst[:, h * HALF_COLS : (h + 1) * HALF_COLS] for h in range(HALVES)]
 
         g1, g2, larger = {}, {}, {}
 
         def pick(q):
-            g2[q] = sbuf([P, J], F32, f"g2_{q}")
-            g1[q] = sbuf([P, J], F32, f"g1_{q}", tag=f"g2_{q - 2}" if q in VECTOR_PLANES or q == last else None)
+            g2[q] = sbuf([P, J], F32, f"g2_{q}", tag=f"g2_{q - 2}" if q == last else None)
+            g1[q] = sbuf([P, J], F32, f"g1_{q}", tag=f"larger{q - 2}" if q == last else None)
             if q == last:
                 for h in range(HALVES):
-                    gather(False, g2[q][:, half[h]], planes[q][:], half_list(list2, h))
-                    gather(h == 0, g1[q][:, half[h]], planes[q][:], half_list(list1, h))
+                    gather(False, g2[q][:, half[h]], planes[q][:], halves_of(list2)[h])
+                for h in range(HALVES):
+                    gather(h == 0, g1[q][:, half[h]], planes[q][:], halves_of(list1)[h])
             else:
                 gather(False, g2[q][:], planes[q][:], list2[:])
-                gather(q in VECTOR_PLANES, g1[q][:], planes[q][:], list1[:])
+                gather(q < VECTOR_PLANES, g1[q][:], planes[q][:], list1[:])
 
         def keep_larger(q, pieces):
-            if q not in larger:
-                larger[q] = sbuf([P, J], F32, f"larger{q}")
+            larger[q] = sbuf([P, J], F32, f"larger{q}")
             for cols in pieces:
                 nc.vector.tensor_tensor(larger[q][:, cols], g1[q][:, cols], g2[q][:, cols], MAX)
 
@@ -169,44 +175,31 @@ def tile_list_largerpicks_plain_floored_kernel(
             for cols in pieces:
                 scale_into(q, cols, larger[q][:, cols])
 
-        pick(0)
-        keep_larger(0, [whole])
-        scale(0, [whole])
-        pick(1)
-        pick(2)
-        keep_larger(1, [whole])
-        keep_larger(2, [whole])
-        scale(1, [whole])
-        scale(2, [whole])
-        pick(3)
-        keep_larger(3, [whole])
-        ws_dealt = sbuf([P, PASSES, R], U8, "ws_dealt", tag="larger2")
-        nc.vector.tensor_copy(
-            out=ws_dealt[:].rearrange("p a (t m) -> p a t m", t=PACK),
-            in_=ws_raw[:].rearrange("p a (m t) -> p a t m", t=PACK),
-        )
-        scale(3, [whole])
-        quantise_u(0, whole)
-        for h in range(HALVES):
-            first_product(0, h, ws_dealt)
-        pick(4)
-        keep_larger(4, [whole])
-        scale(4, [whole])
-        pick(5)
-        keep_larger(5, [whole])
-        scale(5, [whole])
-        pick(6)
-        pick(last)
-        keep_larger(6, [whole])
-        keep_larger(last, half[:1])
-        scale(6, [whole])
-        keep_larger(last, half[1:])
+        for q in range(last):
+            pick(q)
+            keep_larger(q, [whole])
+            if q == last - 1:
+                pick(last)
+            scale(q, [whole])
+            if q == VECTOR_PLANES - 1:
+                ws_dealt = sbuf([P, PASSES, R], U8, "ws_dealt", tag=f"larger{q}")
+                nc.vector.tensor_copy(
+                    out=ws_dealt[:].rearrange("p a (t m) -> p a t m", t=PACK),
+                    in_=ws_raw[:].rearrange("p a (m t) -> p a t m", t=PACK),
+                )
+            if q == last - 2:
+                u_codes[0] = sbuf([P, J], U32, "u_codes0", tag=f"g1_{q}")
+                quantise_u(0, whole)
+                for h in range(HALVES):
+                    first_product(0, h, ws_dealt)
+        keep_larger(last, half)
         scale(last, half)
+        u_codes[1] = sbuf([P, J], U32, "u_codes1")
         for h in range(HALVES):
             quantise_u(PASSES - 1, half[h])
             first_product(PASSES - 1, h, ws_dealt)
 
-        floor = sbuf([P, N_TILES, J], F32, "floor", tag=f"g2_{last - 1}")
+        floor = sbuf([P, N_TILES, J], F32, "floor", tag=f"g2_{last - 2}")
         for n in range(N_TILES):
             gather(False, floor[:, n, :], tz_sb[:, n, :], list3[:])
 
@@ -215,10 +208,6 @@ def tile_list_largerpicks_plain_floored_kernel(
             hid_codes = sbuf([P, JH], U32, f"hid_codes{h}")
             hid_sc = sbuf([P, JH], U8, f"hid_sc{h}")
             nc.scalar.activation(hid_il[:], acc[h][:].rearrange("p t j -> p j t"), RELU)
-            if h == 0:
-                rw_ps = psum.tile([P, HALVES, JH], F32, name="rw_ps", tag="acc0")
-                for c in range(HALVES):
-                    nc.tensor.transpose(rw_ps[:, c, :], rw_col[:, c : c + 1].to_broadcast([P, P]), ident[:])
             nc.vector.quantize_mx(
                 out=hid_codes[:].bitcast(E5M2),
                 scales=hid_sc[:],
@@ -241,6 +230,9 @@ def tile_list_largerpicks_plain_floored_kernel(
             for n in range(N_TILES):
                 nc.vector.tensor_tensor(top[:, n, :], prod[h][n][:], floor[:, n, half[h]], MAX)
             for n in range(N_TILES):
-                nc.vector.tensor_tensor(res[n][:], top[:, n, :], rw_ps[:, h, :], MULT)
+                if h == 0:
+                    nc.gpsimd.tensor_tensor(res[n][:], top[:, n, :], rw_first[:], MULT)
+                else:
+                    nc.vector.tensor_tensor(res[n][:], top[:, n, :], rw_ps[:, h, :], MULT)
                 queue = nc.sync if n == 0 else nc.scalar
                 queue.dma_start(out=out[n * P : (n + 1) * P, half[h]], in_=res[n][:])

@@ -155,32 +155,30 @@ def tile_list_largerpicks_plain_floored_kernel(
         g1, g2, larger = {}, {}, {}
 
         def pick(q):
-            g2[q] = sbuf([P, J], F32, f"g2_{q}", tag=f"g2_{q - 2}" if q == last else None)
-            g1[q] = sbuf([P, J], F32, f"g1_{q}", tag=f"larger{q - 2}" if q == last else None)
-            if q == last:
+            held = q == last
+            g2[q] = sbuf([P, J], F32, f"g2_{q}", tag=f"g2_{q - 2}" if held else None)
+            g1[q] = sbuf([P, J], F32, f"g1_{q}", tag=f"larger{q - 2}" if held else None)
+            if held:
                 for h in range(HALVES):
                     gather(False, g2[q][:, half[h]], planes[q][:], halves_of(list2)[h])
-                for h in range(HALVES):
-                    gather(h == 0, g1[q][:, half[h]], planes[q][:], halves_of(list1)[h])
+                    gather(False, g1[q][:, half[h]], planes[q][:], halves_of(list1)[h])
             else:
                 gather(False, g2[q][:], planes[q][:], list2[:])
                 gather(q < VECTOR_PLANES, g1[q][:], planes[q][:], list1[:])
-
-        def keep_larger(q, pieces):
             larger[q] = sbuf([P, J], F32, f"larger{q}")
-            for cols in pieces:
-                nc.vector.tensor_tensor(larger[q][:, cols], g1[q][:, cols], g2[q][:, cols], MAX)
 
-        def scale(q, pieces):
-            for cols in pieces:
-                scale_into(q, cols, larger[q][:, cols])
+        def keep_larger(q, h):
+            nc.vector.tensor_tensor(larger[q][:, half[h]], g1[q][:, half[h]], g2[q][:, half[h]], MAX)
+
+        def scale(q, h):
+            scale_into(q, half[h], larger[q][:, half[h]])
 
         for q in range(last):
             pick(q)
-            keep_larger(q, [whole])
-            if q == last - 1:
-                pick(last)
-            scale(q, [whole])
+            for h in range(HALVES):
+                keep_larger(q, h)
+            for h in range(HALVES):
+                scale(q, h)
             if q == VECTOR_PLANES - 1:
                 ws_dealt = sbuf([P, PASSES, R], U8, "ws_dealt", tag=f"larger{q}")
                 nc.vector.tensor_copy(
@@ -192,14 +190,18 @@ def tile_list_largerpicks_plain_floored_kernel(
                 quantise_u(0, whole)
                 for h in range(HALVES):
                     first_product(0, h, ws_dealt)
-        keep_larger(last, half)
-        scale(last, half)
         u_codes[1] = sbuf([P, J], U32, "u_codes1")
-        for h in range(HALVES):
-            quantise_u(PASSES - 1, half[h])
-            first_product(PASSES - 1, h, ws_dealt)
+        pick(last)
+        keep_larger(last, 0)
+        scale(last, 0)
+        keep_larger(last, 1)
+        quantise_u(PASSES - 1, half[0])
+        first_product(PASSES - 1, 0, ws_dealt)
+        scale(last, 1)
+        quantise_u(PASSES - 1, half[1])
+        first_product(PASSES - 1, 1, ws_dealt)
 
-        floor = sbuf([P, N_TILES, J], F32, "floor", tag=f"g2_{last - 2}")
+        floor = sbuf([P, N_TILES, J], F32, "floor", tag=f"plane{last}")
         for n in range(N_TILES):
             gather(False, floor[:, n, :], tz_sb[:, n, :], list3[:])
 

@@ -70,8 +70,8 @@ def tile_list_largerpicks_plain_floored_kernel(
 
         def load_w_scales(quad):
             nc.sync.dma_start(
-                out=ws_raw[32 * quad : 32 * quad + 4].bitcast(I32),
-                in_=w_scales[:, 4 * quad : 4 * quad + 4, :].rearrange("a r c -> r a c").bitcast(I32),
+                out=ws_raw[quad:P:32].bitcast(I32),
+                in_=w_scales[:, quad:16:4, :].rearrange("a r c -> r a c").bitcast(I32),
             )
 
         nc.sync.dma_start(out=w_raw[:].bitcast(I32), in_=w_words.rearrange("a p c -> p a c").bitcast(I32))
@@ -93,8 +93,8 @@ def tile_list_largerpicks_plain_floored_kernel(
         )
         for quad in range(4):
             nc.sync.dma_start(
-                out=wb_sc[32 * quad : 32 * quad + 4, :].bitcast(I32),
-                in_=wb_scales[0, 4 * quad : 4 * quad + 4, :].bitcast(I32),
+                out=wb_sc[quad:P:32, :].bitcast(I32),
+                in_=wb_scales[0, quad:16:4, :].bitcast(I32),
             )
 
         nc.vector.tensor_copy(
@@ -161,7 +161,7 @@ def tile_list_largerpicks_plain_floored_kernel(
             if held:
                 for h in range(HALVES):
                     gather(False, g2[q][:, half[h]], planes[q][:], halves_of(list2)[h])
-                    gather(False, g1[q][:, half[h]], planes[q][:], halves_of(list1)[h])
+                    gather(h == 1, g1[q][:, half[h]], planes[q][:], halves_of(list1)[h])
             else:
                 gather(False, g2[q][:], planes[q][:], list2[:])
                 gather(q < VECTOR_PLANES, g1[q][:], planes[q][:], list1[:])
@@ -175,6 +175,8 @@ def tile_list_largerpicks_plain_floored_kernel(
 
         for q in range(last):
             pick(q)
+            if q == last - 1:
+                pick(last)
             for h in range(HALVES):
                 keep_larger(q, h)
             for h in range(HALVES):
@@ -191,15 +193,13 @@ def tile_list_largerpicks_plain_floored_kernel(
                 for h in range(HALVES):
                     first_product(0, h, ws_dealt)
         u_codes[1] = sbuf([P, J], U32, "u_codes1")
-        pick(last)
-        keep_larger(last, 0)
-        scale(last, 0)
-        keep_larger(last, 1)
-        quantise_u(PASSES - 1, half[0])
-        first_product(PASSES - 1, 0, ws_dealt)
-        scale(last, 1)
-        quantise_u(PASSES - 1, half[1])
-        first_product(PASSES - 1, 1, ws_dealt)
+        for h in range(HALVES):
+            keep_larger(last, h)
+        for h in range(HALVES):
+            scale(last, h)
+        for h in range(HALVES):
+            quantise_u(PASSES - 1, half[h])
+            first_product(PASSES - 1, h, ws_dealt)
 
         floor = sbuf([P, N_TILES, J], F32, "floor", tag=f"plane{last}")
         for n in range(N_TILES):

from contextlib import ExitStack

import concourse.mybir as mybir
from concourse.masks import make_identity

K, T, J, R, N, Z = 1024, 1024, 256, 512, 256, 512
FLOPS = 2 * K * R * J + 2 * R * N * J

F32 = mybir.dt.float32
BF16 = mybir.dt.bfloat16
I32 = mybir.dt.int32
U32 = mybir.dt.uint32
U16 = mybir.dt.uint16
U8 = mybir.dt.uint8
E4M3 = mybir.dt.float8_e4m3fn_x4
E5M2 = mybir.dt.float8_e5m2_x4
E2M1 = mybir.dt.float4_e2m1fn_x4
MAX = mybir.AluOpType.max
MULT = mybir.AluOpType.mult
COPY = mybir.ActivationFunctionType.Copy
RELU = mybir.ActivationFunctionType.Relu

P = 128
PACK = 4
PASSES = K // (P * PACK)
HALVES = 2
JH = J // HALVES
LIST_COLS = J // 16
HALF_COLS = JH // 16
N_TILES = N // P
VECTOR_PLANES = 2


def tile_list_largerpicks_plain_floored_kernel(
    tc, xf, fk, w_words, w_scales, wb_words, wb_scales, tz, rw, offs, offs2, offs3, out
):
    nc = tc.nc
    with ExitStack() as ctx:
        keep = ctx.enter_context(tc.tile_pool(name="keep", bufs=1))
        psum = ctx.enter_context(tc.psum_pool(name="psum", bufs=1))

        def sbuf(shape, dtype, name, tag=None):
            return keep.tile(shape, dtype, name=name, tag=tag or name, align_bytes=64)

        list1 = sbuf([P, LIST_COLS], U16, "list1")
        list2 = sbuf([P, LIST_COLS], U16, "list2")
        list3 = sbuf([P, LIST_COLS], U16, "list3")
        w_raw = sbuf([P, PASSES, 2 * R], U8, "w_raw")
        ws_raw = sbuf([P, PASSES, R], U8, "ws_raw")
        w_dealt = sbuf([P, PASSES, 2 * R], U8, "w_dealt")
        wb_codes = sbuf([P, N], U32, "wb_codes")
        wb_sc = sbuf([P, N], U8, "wb_sc")
        fk_sb = sbuf([P, PASSES, PACK], F32, "fk_sb")
        rw_col = sbuf([P, 2], F32, "rw_col")
        ident = sbuf([P, P], F32, "ident")
        planes = [sbuf([P, T], F32, f"plane{q}") for q in range(PASSES * PACK)]
        tz_sb = sbuf([P, N_TILES, Z], F32, "tz_sb")

        nc.gpsimd.memset(ws_raw[:].rearrange("p a r -> p (a r)").bitcast(I32), 0)
        nc.vector.memset(wb_sc[:].bitcast(I32), 0)
        warm = sbuf([P, 8], F32, "warm")
        nc.vector.memset(warm[:, 0:4], 0.0)
        nc.scalar.activation(warm[:, 4:8], warm[:, 0:4], COPY)
        make_identity(nc, ident[:])

        x_rows = xf.rearrange("(a p i) t -> a i p t", p=P, i=PACK)

        def load_plane(q):
            nc.sync.dma_start(out=planes[q][:], in_=x_rows[q // PACK, q % PACK])

        def load_w_scales(quad):
            nc.sync.dma_start(
                out=ws_raw[quad:P:32].bitcast(I32),
                in_=w_scales[:, quad:16:4, :].rearrange("a r c -> r a c").bitcast(I32),
            )

        nc.sync.dma_start(out=w_raw[:].bitcast(I32), in_=w_words.rearrange("a p c -> p a c").bitcast(I32))
        nc.sync.dma_start(list1[:], offs)
        nc.sync.dma_start(list2[:], offs2)
        nc.scalar.dma_start(out=fk_sb[:], in_=fk.rearrange("(a p i) o -> p a (i o)", p=P, i=PACK))
        with nc.allow_non_contiguous_dma(reason="one weight to a partition"):
            nc.scalar.dma_start(out=rw_col[:], in_=rw.rearrange("o (h p) -> p (o h)", p=P))
        for q in range(3):
            load_plane(q)
        for quad in range(4):
            load_w_scales(quad)
        for q in range(3, PASSES * PACK):
            load_plane(q)
        nc.sync.dma_start(list3[:], offs3)
        nc.sync.dma_start(out=tz_sb[:], in_=tz.rearrange("(n p) z -> p n z", p=P))
        nc.sync.dma_start(
            out=wb_codes[:].bitcast(I32), in_=wb_words[0].rearrange("p n t -> p (n t)").bitcast(I32)
        )
        for quad in range(4):
            nc.sync.dma_start(
                out=wb_sc[quad:P:32, :].bitcast(I32),
                in_=wb_scales[0, quad:16:4, :].bitcast(I32),
            )

        nc.vector.tensor_copy(
            out=w_dealt[:].bitcast(U16).rearrange("p a (t m) -> p a t m", t=PACK),
            in_=w_raw[:].bitcast(U16).rearrange("p a (m t) -> p a t m", t=PACK),
        )

        acc = [psum.tile([P, PACK, JH], F32, name=f"acc{h}") for h in range(HALVES)]
        prod = [[psum.tile([P, JH], F32, name=f"prod{h}_{n}") for n in range(N_TILES)] for h in range(HALVES)]

        rw_ps = psum.tile([P, HALVES, JH], F32, name="rw_ps")
        for h in range(HALVES):
            nc.tensor.transpose(rw_ps[:, h, :], rw_col[:, h : h + 1].to_broadcast([P, P]), ident[:])

        rw_first = sbuf([P, JH], F32, "rw_first")
        nc.scalar.copy(rw_first[:], rw_ps[:, 0, :])

        u_il = [sbuf([P, J * PACK], BF16, f"u_il{a}") for a in range(PASSES)]
        u_codes = {}
        u_sc = [sbuf([P, J], U8, f"u_sc{a}") for a in range(PASSES)]

        def gather(on_vector, dst, window, offsets):
            if on_vector:
                nc.vector.tensor_copy(dst, window.indirect(offsets))
            else:
                nc.scalar.activation(dst, window.indirect(offsets), COPY)

        def scale_into(q, cols, larger):
            a, i = divmod(q, PACK)
            dst = u_il[a][:].rearrange("p (j i) -> p j i", i=PACK)[:, cols, i]
            nc.vector.tensor_scalar_mul(dst, larger, fk_sb[:, a, i : i + 1])

        def quantise_u(a, cols):
            nc.vector.quantize_mx(
                out=u_codes[a][:, cols].bitcast(E4M3),
                scales=u_sc[a][:, cols],
                in_=u_il[a][:, cols.start * PACK : cols.stop * PACK],
            )

        def first_product(a, h, ws_dealt):
            for t in range(PACK):
                nc.tensor.matmul_mx(
                    out=acc[h][:, t, :],
                    lhsT=w_dealt[:, a, 2 * P * t : 2 * P * (t + 1)].bitcast(E2M1),
                    lhsT_scale=ws_dealt[:, a, P * t : P * (t + 1)],
                    rhs=u_codes[a][:, half[h]].bitcast(E4M3),
                    rhs_scale=u_sc[a][:, half[h]],
                    start=(a == 0 and t == 0),
                    stop=(a == PASSES - 1 and t == PACK - 1),
                )

        half = [slice(h * JH, (h + 1) * JH) for h in range(HALVES)]
        whole = slice(0, J)
        last = PASSES * PACK - 1
        def halves_of(lst):
            return [lst[:, h * HALF_COLS : (h + 1) * HALF_COLS] for h in range(HALVES)]

        g1, g2, larger = {}, {}, {}

        def pick(q):
            held = q == last
            g2[q] = sbuf([P, J], F32, f"g2_{q}", tag=f"g2_{q - 2}" if held else None)
            g1[q] = sbuf([P, J], F32, f"g1_{q}", tag=f"larger{q - 2}" if held else None)
            if held:
                for h in range(HALVES):
                    gather(False, g2[q][:, half[h]], planes[q][:], halves_of(list2)[h])
                    gather(h == 1, g1[q][:, half[h]], planes[q][:], halves_of(list1)[h])
            else:
                gather(False, g2[q][:], planes[q][:], list2[:])
                gather(q < VECTOR_PLANES, g1[q][:], planes[q][:], list1[:])
            larger[q] = sbuf([P, J], F32, f"larger{q}")

        def keep_larger(q, h):
            nc.vector.tensor_tensor(larger[q][:, half[h]], g1[q][:, half[h]], g2[q][:, half[h]], MAX)

        def scale(q, h):
            scale_into(q, half[h], larger[q][:, half[h]])

        for q in range(last):
            pick(q)
            if q == last - 1:
                pick(last)
            for h in range(HALVES):
                keep_larger(q, h)
            for h in range(HALVES):
                scale(q, h)
            if q == VECTOR_PLANES - 1:
                ws_dealt = sbuf([P, PASSES, R], U8, "ws_dealt", tag=f"larger{q}")
                nc.vector.tensor_copy(
                    out=ws_dealt[:].rearrange("p a (t m) -> p a t m", t=PACK),
                    in_=ws_raw[:].rearrange("p a (m t) -> p a t m", t=PACK),
                )
            if q == last - 2:
                u_codes[0] = sbuf([P, J], U32, "u_codes0", tag=f"g1_{q}")
                quantise_u(0, whole)
                for h in range(HALVES):
                    first_product(0, h, ws_dealt)
        u_codes[1] = sbuf([P, J], U32, "u_codes1")
        for h in range(HALVES):
            keep_larger(last, h)
        for h in range(HALVES):
            scale(last, h)
        for h in range(HALVES):
            quantise_u(PASSES - 1, half[h])
            first_product(PASSES - 1, h, ws_dealt)

        floor = sbuf([P, N_TILES, J], F32, "floor", tag=f"plane{last}")
        for n in range(N_TILES):
            gather(False, floor[:, n, :], tz_sb[:, n, :], list3[:])

        for h in range(HALVES):
            hid_il = sbuf([P, JH, PACK], BF16, f"hid_il{h}")
            hid_codes = sbuf([P, JH], U32, f"hid_codes{h}")
            hid_sc = sbuf([P, JH], U8, f"hid_sc{h}")
            nc.scalar.activation(hid_il[:], acc[h][:].rearrange("p t j -> p j t"), RELU)
            nc.vector.quantize_mx(
                out=hid_codes[:].bitcast(E5M2),
                scales=hid_sc[:],
                in_=hid_il[:].rearrange("p j t -> p (j t)"),
            )
            for n in range(N_TILES):
                nc.tensor.matmul_mx(
                    out=prod[h][n][:],
                    lhsT=wb_codes[:, n * P : (n + 1) * P].bitcast(E4M3),
                    lhsT_scale=wb_sc[:, n * P : (n + 1) * P],
                    rhs=hid_codes[:].bitcast(E5M2),
                    rhs_scale=hid_sc[:],
                    start=True,
                    stop=True,
                )

        for h in range(HALVES):
            top = sbuf([P, N_TILES, JH], F32, f"top{h}")
            res = [sbuf([P, JH], F32, f"res{h}_{n}") for n in range(N_TILES)]
            for n in range(N_TILES):
                nc.vector.tensor_tensor(top[:, n, :], prod[h][n][:], floor[:, n, half[h]], MAX)
            for n in range(N_TILES):
                if h == 0:
                    nc.gpsimd.tensor_tensor(res[n][:], top[:, n, :], rw_first[:], MULT)
                else:
                    nc.vector.tensor_tensor(res[n][:], top[:, n, :], rw_ps[:, h, :], MULT)
                queue = nc.sync if n == 0 else nc.scalar
                queue.dma_start(out=out[n * P : (n + 1) * P, half[h]], in_=res[n][:])
